import numpy as np
import ml_dtypes


def mxq(x, axis, fmt="e4m3"):
    dtype, down = {"e4m3": (ml_dtypes.float8_e4m3fn, 7), "e5m2": (ml_dtypes.float8_e5m2, 14)}[fmt]
    v = np.moveaxis(np.asarray(x, np.float32).astype(ml_dtypes.bfloat16).astype(np.float64), axis, -1)
    blocks = v.reshape(v.shape[:-1] + (-1, 32))
    amax = np.abs(blocks).max(-1, keepdims=True)
    byte = np.maximum(np.where(amax > 0, np.frexp(amax)[1] - 1 + 127, 0) - down, 1)
    scale = np.exp2(byte - 127.0)
    codes = (blocks / scale).astype(np.float32).astype(dtype).astype(np.float64)
    return np.moveaxis((codes * scale).reshape(v.shape), -1, axis)


WIDE = False


def mx_kscale(k):
    if not WIDE:
        return np.ones(k)
    levels = np.array([10, -10, 5, -5, 0])
    if k % 512:
        return np.exp2(np.random.permutation(np.resize(levels, k // 32))).repeat(32)
    a = np.empty((k // 512, 16))
    for p in range(k // 512):
        a[p, :8] = np.random.permutation(np.resize(levels, 8))
        for g in range(8):
            far = levels[np.abs(levels - a[p, g]) >= 10]
            a[p, g + 8] = far[np.random.randint(len(far))]
    return np.exp2(a.ravel()).repeat(32)


def f64(x):
    return np.asarray(x).astype(np.float64)


def striped(idx):
    return np.tile(np.asarray(idx).reshape(-1, 16).T, (8, 1)).astype(np.uint16)


def unstriped(offs):
    return offs[:16].T.reshape(-1).astype(np.int64)


E2M1 = np.array([0.0, 0.5, 1.0, 1.5, 2.0, 3.0, 4.0, 6.0, -0.0, -0.5, -1.0, -1.5, -2.0, -3.0, -4.0, -6.0])


def pack_weight(w, fmt):
    k, n = w.shape
    w = f64(np.asarray(w, np.float32).astype(ml_dtypes.bfloat16)).reshape(k // 32, 32, n)
    amax = np.abs(w).max(1)
    if fmt == "e4m3":
        byte = np.frexp(amax)[1] - 1 + 127 - 7
    else:
        mant, ex = np.frexp(amax / 6.0)
        byte = np.where(mant > 0.5, ex, ex - 1) + 127
    byte = np.clip(np.where(amax > 0, byte, 1), 1, 254)
    scaled = (w * np.exp2(127.0 - byte)[:, None, :]).reshape(k, n).astype(np.float32)
    by_word = np.ascontiguousarray(scaled.reshape(k // 512, 128, 4, n).transpose(0, 1, 3, 2))
    if fmt == "e4m3":
        words = by_word.astype(ml_dtypes.float8_e4m3fn).view(np.uint8)
    else:
        c = by_word.astype(ml_dtypes.float4_e2m1fn).view(np.uint8) & 0xF
        words = (c[..., 0::2] | (c[..., 1::2] << 4)).reshape(k // 512, 128, 2 * n)
    return np.ascontiguousarray(words), np.ascontiguousarray(byte.astype(np.uint8).reshape(k // 512, 16, n))


def unpack_weight(words, scales, fmt):
    g, _, n = scales.shape
    words = np.ascontiguousarray(words).reshape(g, 128, n, -1)
    if fmt == "e4m3":
        vals = words.view(ml_dtypes.float8_e4m3fn).astype(np.float64)
    else:
        nib = np.empty((g, 128, n, 4), np.uint8)
        nib[..., 0::2] = words & 0xF
        nib[..., 1::2] = words >> 4
        vals = E2M1[nib]
    vals = vals * np.repeat(np.exp2(scales.astype(np.float64) - 127.0), 8, axis=1)[..., None]
    return vals.transpose(0, 1, 3, 2).reshape(g * 512, n)


def sigmoid(v):
    return 1.0 / (1.0 + np.exp(-v))


D, E, T, I, Q = 512, 512, 1024, 256, 512


def setup_inputs():
    n = np.random.standard_normal
    idx = np.random.permutation(T)[:I]
    fd = mx_kscale(D)
    fq = mx_kscale(Q)
    keysp = pack_weight(n((D, T)) / fd[:, None], "e2m1")
    return {
        "query": (n((D, Q)) * 0.5 / np.sqrt(D) * fd[:, None]).astype(np.float32),
        "qs": (np.random.uniform(8.0, 32.0, (Q, 1)) * fq[:, None]).astype(np.float32),
        "grows": (n((Q, E)) / fq[:, None]).astype(np.float32),
        "vals": (n((E, T))).astype(np.float32),
        "keys_words": keysp[0],
        "keys_scales": keysp[1],
        "gates": (n((E, T))).astype(np.float32),
        "gb": (np.random.uniform(-0.5, 0.5, (E, 1))).astype(np.float32),
        "sg": (np.random.uniform(0.5, 2.0, (1, I))).astype(np.float32),
        "old": (n((E, T)) * 1.0).astype(np.float32),
        "fade": (np.random.uniform(0.5, 1.0, (1, T))).astype(np.float32),
        "offs": striped(idx),
    }


def reference(query, qs, grows, vals, keys_words, keys_scales, gates, gb, sg, old, fade, offs):
    idx = unstriped(offs)
    keysu = unpack_weight(keys_words, keys_scales, "e2m1")
    queryq = mxq(f64(query), 0, "e4m3")
    keysidxg = keysu[:, idx]
    a = queryq.T @ keysidxg
    p = np.exp(a - np.max(a, axis=1, keepdims=True))
    w = p * f64(qs) / np.sum(p, axis=1, keepdims=True)
    growsq = mxq(f64(grows), 0, "e4m3")
    wq = mxq(w, 0, "e4m3")
    c0 = growsq.T @ wq
    x1 = f64(gates)[:, idx] + f64(gb)
    g1 = sigmoid(x1)
    dg1 = c0 * f64(vals)[:, idx]
    dx1 = dg1 * g1 * (1.0 - g1)
    gs = dx1 * f64(sg)
    gf = np.zeros((E, T))
    gf[:, idx] = gs
    y = f64(old) * f64(fade) + gf
    return y

@@ -1,0 +1,198 @@
+from contextlib import ExitStack
+
+import concourse.mybir as mybir
+from concourse.masks import make_identity
+
+D, E, T, I, Q = 512, 512, 1024, 256, 512
+FLOPS = 2 * D * Q * I + 2 * Q * E * I
+
+F32 = mybir.dt.float32
+BF16 = mybir.dt.bfloat16
+I32 = mybir.dt.int32
+U32 = mybir.dt.uint32
+U16 = mybir.dt.uint16
+U8 = mybir.dt.uint8
+FP8X4 = mybir.dt.float8_e4m3fn_x4
+FP4X4 = mybir.dt.float4_e2m1fn_x4
+ALU = mybir.AluOpType
+ACT = mybir.ActivationFunctionType
+AX = mybir.AxisListType
+
+P = 128
+PACK = 4
+BANK = 512
+E_TILES = E // P
+T_BLOCKS = T // P
+FADE_ROW, GB_ROW, SG_ROW, VEC_ROWS = 0, 8, 12, 16
+
+
+def tile_attend_bvgatedby_s_kernel(tc, query, qs, grows, vals, keys_words, keys_scales, gates, gb, sg, old, fade, offs, out):
+    nc = tc.nc
+    with ExitStack() as ctx:
+        keep = ctx.enter_context(tc.tile_pool(name="keep", bufs=1))
+        ring = ctx.enter_context(tc.tile_pool(name="ring", bufs=2))
+        psum = ctx.enter_context(tc.psum_pool(name="psum", bufs=1))
+
+        def bank(n, name):
+            return psum.tile([P, BANK], F32, tag="bank%d" % n, name=name)
+
+        key_scales = keep.tile([P, T], U8, align_bytes=64)
+        nc.vector.memset(key_scales[:].bitcast(I32), 0)
+        ident = keep.tile([P, P], F32)
+        vec_rows = keep.tile([P, P], F32)
+        nc.gpsimd.memset(vec_rows[:], 0.0)
+        make_identity(nc, ident[:])
+        warm_in = keep.tile([P, 1], F32)
+        nc.vector.memset(warm_in[:], 0.0)
+        warm = keep.tile([P, 1], F32)
+        nc.scalar.activation(warm[:], warm_in[:], ACT.Exp)
+
+        offsets = keep.tile([P, I // 16], U16, name="offsets")
+        nc.sync.dma_start(offsets[:], offs)
+        key_words = keep.tile([P, T], U16, align_bytes=64)
+        nc.sync.dma_start(key_words[:].bitcast(I32), keys_words[0].bitcast(I32))
+        for quad in range(4):
+            nc.scalar.dma_start(key_scales[32 * quad : 32 * quad + 4, :].bitcast(I32),
+                                keys_scales[0, 4 * quad : 4 * quad + 4, :].bitcast(I32))
+        query_rows = query.rearrange("(p j) q -> p j q", j=PACK)
+        query_raw = []
+        for h in range(2):
+            raw = keep.tile([P, PACK, Q // 2], F32, name="query_raw%d" % h)
+            nc.sync.dma_start(raw[:], query_rows[:, :, h * (Q // 2) : (h + 1) * (Q // 2)])
+            query_raw.append(raw)
+        grows_rows = grows.rearrange("(p j) e -> p j e", j=PACK)
+        grows_raw = []
+        for h in range(2):
+            raw = keep.tile([P, PACK, E // 2], F32, name="grows_raw%d" % h)
+            nc.sync.dma_start(raw[:], grows_rows[:, :, h * (E // 2) : (h + 1) * (E // 2)])
+            grows_raw.append(raw)
+        row_scale = keep.tile([P, PACK], F32)
+        nc.gpsimd.dma_start(row_scale[:], qs.rearrange("(p r) o -> p (r o)", r=PACK))
+        nc.gpsimd.dma_start(vec_rows[SG_ROW : SG_ROW + I // P, :], sg.rearrange("o (c p) -> (o c) p", p=P))
+        nc.gpsimd.dma_start(vec_rows[GB_ROW : GB_ROW + E_TILES, :], gb.rearrange("(c p) o -> c (p o)", p=P))
+        nc.gpsimd.dma_start(vec_rows[FADE_ROW : FADE_ROW + T_BLOCKS, :], fade.rearrange("o (c p) -> (o c) p", p=P))
+        gates_sb, vals_sb, old_sb = [], [], []
+        for k in range(E_TILES):
+            rows = slice(k * P, (k + 1) * P)
+            for name, src, held in (("gates", gates, gates_sb), ("vals", vals, vals_sb), ("old", old, old_sb)):
+                pool_tile = keep.tile([P, T], F32, name="%s%d" % (name, k))
+                nc.sync.dma_start(pool_tile[:], src[rows, :])
+                held.append(pool_tile)
+
+        window = keep.tile([P, T], F32)
+        nc.vector.memset(window[:], 0.0)
+
+        listed_words = keep.tile([P, I], U16, align_bytes=64)
+        listed_scales = keep.tile([P, I], U8, align_bytes=64)
+        nc.vector.tensor_copy(listed_words[:], key_words[:].indirect(offsets[:]))
+        nc.vector.tensor_copy(listed_scales[:], key_scales[:].indirect(offsets[:]))
+
+        query_bf = keep.tile([P, PACK, P, PACK], BF16, align_bytes=64)
+        half_s = P // 2
+        for h, copy in enumerate((nc.scalar.copy, nc.vector.tensor_copy)):
+            copy(query_bf[:, :, h * half_s : (h + 1) * half_s, :].rearrange("p r s j -> p s j r"),
+                 query_raw[h][:].rearrange("p j (s r) -> p s j r", r=PACK))
+        query_codes = keep.tile([P, Q], U32, align_bytes=64)
+        query_scales = keep.tile([P, Q], U8, align_bytes=64)
+        for r in range(PACK):
+            cols = slice(r * P, (r + 1) * P)
+            nc.vector.quantize_mx(query_codes[:, cols].bitcast(FP8X4), query_scales[:, cols],
+                                  query_bf[:, r, :, :].rearrange("p s j -> p (s j)"))
+
+        grows_bf = keep.tile([P, E, PACK], BF16, align_bytes=64)
+        grows_codes = keep.tile([P, E], U32, align_bytes=64)
+        grows_scales = keep.tile([P, E], U8, align_bytes=64)
+
+        def cast_grows(k):
+            src = grows_raw[k // 2][:, :, (k % 2) * P : (k % 2 + 1) * P]
+            nc.scalar.copy(grows_bf[:, k * P : (k + 1) * P, :].rearrange("p (c i) j -> p c j i", i=4),
+                           src.rearrange("p j (c i) -> p c j i", i=4))
+
+        def quantize_grows(k):
+            cols = slice(k * P, (k + 1) * P)
+            nc.vector.quantize_mx(grows_codes[:, cols].bitcast(FP8X4), grows_scales[:, cols],
+                                  grows_bf[:, cols, :].rearrange("p e j -> p (e j)"))
+
+        cast_grows(0)
+        cast_grows(1)
+
+        neg_max = keep.tile([P, PACK], F32)
+        row_sum = keep.tile([P, PACK], F32)
+        inv_sum = keep.tile([P, PACK], F32)
+        probs = keep.tile([P, PACK, I], F32)
+        w_planes = keep.tile([P, PACK, I], BF16)
+        scores = []
+        for r in range(PACK):
+            cols = slice(r * P, (r + 1) * P)
+            score = bank(4 + r, "score%d" % r)
+            nc.tensor.matmul_mx(score[:, :I], lhsT=query_codes[:, cols].bitcast(FP8X4), lhsT_scale=query_scales[:, cols],
+                                rhs=listed_words[:].bitcast(FP4X4), rhs_scale=listed_scales[:], start=True, stop=True)
+            scores.append(score)
+        for r in range(PACK):
+            nc.vector.tensor_reduce(neg_max[:, r : r + 1], scores[r][:, :I], AX.X, ALU.max, negate=True)
+            nc.scalar.activation(probs[:, r, :], scores[r][:, :I], ACT.Exp, bias=neg_max[:, r : r + 1],
+                                 accum_out=row_sum[:, r : r + 1])
+        for r in range(PACK):
+            nc.vector.reciprocal(inv_sum[:, r : r + 1], row_sum[:, r : r + 1])
+            if r < 2:
+                quantize_grows(r)
+            nc.vector.tensor_scalar(w_planes[:, r, :], probs[:, r, :], inv_sum[:, r : r + 1], row_scale[:, r : r + 1],
+                                    ALU.mult, ALU.mult)
+        w_bf = keep.tile([P, I, PACK], BF16, align_bytes=64)
+        nc.vector.tensor_copy(w_bf[:].rearrange("p (c i) r -> p c r i", i=4),
+                              w_planes[:].rearrange("p r (c i) -> p c r i", i=4))
+        w_codes = keep.tile([P, I], U32, align_bytes=64)
+        w_scales = keep.tile([P, I], U8, align_bytes=64)
+        nc.vector.quantize_mx(w_codes[:].bitcast(FP8X4), w_scales[:], w_bf[:].rearrange("p i r -> p (i r)"))
+
+        turned = bank(7, "turned")
+        nc.tensor.transpose(turned[:, :P], vec_rows[:], ident[:])
+        vec_cols = keep.tile([P, VEC_ROWS], F32)
+        nc.scalar.copy(vec_cols[:], turned[:, :VEC_ROWS])
+        spread = bank(3, "spread")
+        for c in range(I // P):
+            nc.tensor.transpose(spread[:, c * P : (c + 1) * P],
+                                vec_cols[:, SG_ROW + c : SG_ROW + c + 1].to_broadcast([P, P]), ident[:])
+        neg_gain = keep.tile([P, I], F32)
+        nc.scalar.activation(neg_gain[:], spread[:, :I], ACT.Copy, scale=-0.25)
+        half_bias = keep.tile([P, E_TILES], F32)
+        nc.scalar.activation(half_bias[:], turned[:, GB_ROW : GB_ROW + E_TILES], ACT.Copy, scale=0.5)
+
+        for k in range(E_TILES):
+            cols = slice(k * P, (k + 1) * P)
+            if k >= 2:
+                cast_grows(k)
+                quantize_grows(k)
+            c0 = bank(k % 2, "c0_%d" % k)
+            nc.tensor.matmul_mx(c0[:, :I], lhsT=grows_codes[:, cols].bitcast(FP8X4), lhsT_scale=grows_scales[:, cols],
+                                rhs=w_codes[:].bitcast(FP8X4), rhs_scale=w_scales[:], start=True, stop=True)
+            listed_gates = ring.tile([P, I], F32, name="listed_gates")
+            nc.vector.tensor_copy(listed_gates[:], gates_sb[k][:].indirect(offsets[:]))
+            tanh_half = ring.tile([P, I], F32, name="tanh_half")
+            nc.scalar.activation(tanh_half[:], listed_gates[:], ACT.Tanh, bias=half_bias[:, k : k + 1], scale=0.5)
+            centred = ring.tile([P, I], F32, name="centred")
+            nc.scalar.activation(centred[:], tanh_half[:], ACT.Square)
+            gained = ring.tile([P, I], F32, name="gained")
+            nc.vector.tensor_tensor(gained[:], vals_sb[k][:].indirect(offsets[:]), neg_gain[:], ALU.mult)
+            chained = ring.tile([P, I], F32, name="chained")
+            nc.vector.scalar_tensor_tensor(chained[:], centred[:], -1.0, c0[:, :I], ALU.add, ALU.mult)
+            nc.vector.tensor_tensor(window[:].indirect(offsets[:]), gained[:], chained[:], ALU.mult)
+
+            faded_t = ring.tile([P, T_BLOCKS, P], F32, name="faded_t")
+            for half in range(2):
+                old_t = bank(2 + half, "old_t%d_%d" % (k, half))
+                for c in range(4):
+                    blk = 4 * half + c
+                    nc.tensor.transpose(old_t[:, c * P : (c + 1) * P], old_sb[k][:, blk * P : (blk + 1) * P], ident[:])
+                for c in range(4):
+                    blk = 4 * half + c
+                    nc.scalar.activation(faded_t[:, blk, :], old_t[:, c * P : (c + 1) * P], ACT.Copy,
+                                         scale=vec_cols[:, FADE_ROW + blk : FADE_ROW + blk + 1])
+            for half in range(2):
+                faded = bank(4 + 2 * (k % 2) + half, "faded%d_%d" % (k, half))
+                for c in range(4):
+                    nc.tensor.transpose(faded[:, c * P : (c + 1) * P], faded_t[:, 4 * half + c, :], ident[:])
+                result = keep.tile([P, BANK], F32, name="result%d_%d" % (k, half))
+                t_cols = slice(half * BANK, (half + 1) * BANK)
+                nc.vector.tensor_tensor(result[:], faded[:], window[:, t_cols], ALU.add)
+                nc.sync.dma_start(out[cols, t_cols], result[:])

@@ -37,22 +37,18 @@ def tile_attend_bvgatedby_s_kernel(tc, query, qs, grows, vals, keys_words, keys_
             return psum.tile([P, BANK], F32, tag="bank%d" % n, name=name)
 
         key_scales = keep.tile([P, T], U8, align_bytes=64)
-        nc.vector.memset(key_scales[:].bitcast(I32), 0)
+        nc.gpsimd.memset(key_scales[:].bitcast(I32), 0)
         ident = keep.tile([P, P], F32)
         vec_rows = keep.tile([P, P], F32)
         nc.gpsimd.memset(vec_rows[:], 0.0)
         make_identity(nc, ident[:])
-        warm_in = keep.tile([P, 1], F32)
-        nc.vector.memset(warm_in[:], 0.0)
-        warm = keep.tile([P, 1], F32)
-        nc.scalar.activation(warm[:], warm_in[:], ACT.Exp)
 
         offsets = keep.tile([P, I // 16], U16, name="offsets")
         nc.sync.dma_start(offsets[:], offs)
         key_words = keep.tile([P, T], U16, align_bytes=64)
         nc.sync.dma_start(key_words[:].bitcast(I32), keys_words[0].bitcast(I32))
         for quad in range(4):
-            nc.scalar.dma_start(key_scales[32 * quad : 32 * quad + 4, :].bitcast(I32),
+            nc.sync.dma_start(key_scales[32 * quad : 32 * quad + 4, :].bitcast(I32),
                                 keys_scales[0, 4 * quad : 4 * quad + 4, :].bitcast(I32))
         query_rows = query.rearrange("(p j) q -> p j q", j=PACK)
         query_raw = []
@@ -67,10 +63,10 @@ def tile_attend_bvgatedby_s_kernel(tc, query, qs, grows, vals, keys_words, keys_
             nc.sync.dma_start(raw[:], grows_rows[:, :, h * (E // 2) : (h + 1) * (E // 2)])
             grows_raw.append(raw)
         row_scale = keep.tile([P, PACK], F32)
-        nc.gpsimd.dma_start(row_scale[:], qs.rearrange("(p r) o -> p (r o)", r=PACK))
-        nc.gpsimd.dma_start(vec_rows[SG_ROW : SG_ROW + I // P, :], sg.rearrange("o (c p) -> (o c) p", p=P))
-        nc.gpsimd.dma_start(vec_rows[GB_ROW : GB_ROW + E_TILES, :], gb.rearrange("(c p) o -> c (p o)", p=P))
-        nc.gpsimd.dma_start(vec_rows[FADE_ROW : FADE_ROW + T_BLOCKS, :], fade.rearrange("o (c p) -> (o c) p", p=P))
+        nc.sync.dma_start(row_scale[:], qs.rearrange("(p r) o -> p (r o)", r=PACK))
+        nc.sync.dma_start(vec_rows[SG_ROW : SG_ROW + I // P, :], sg.rearrange("o (c p) -> (o c) p", p=P))
+        nc.sync.dma_start(vec_rows[GB_ROW : GB_ROW + E_TILES, :], gb.rearrange("(c p) o -> c (p o)", p=P))
+        nc.sync.dma_start(vec_rows[FADE_ROW : FADE_ROW + T_BLOCKS, :], fade.rearrange("o (c p) -> (o c) p", p=P))
         gates_sb, vals_sb, old_sb = [], [], []
         for k in range(E_TILES):
             rows = slice(k * P, (k + 1) * P)
@@ -89,9 +85,10 @@ def tile_attend_bvgatedby_s_kernel(tc, query, qs, grows, vals, keys_words, keys_
 
         query_bf = keep.tile([P, PACK, P, PACK], BF16, align_bytes=64)
         half_s = P // 2
-        for h, copy in enumerate((nc.scalar.copy, nc.vector.tensor_copy)):
-            copy(query_bf[:, :, h * half_s : (h + 1) * half_s, :].rearrange("p r s j -> p s j r"),
-                 query_raw[h][:].rearrange("p j (s r) -> p s j r", r=PACK))
+        dealt = [(query_bf[:, :, h * half_s : (h + 1) * half_s, :].rearrange("p r s j -> p s j r"),
+                  query_raw[h][:].rearrange("p j (s r) -> p s j r", r=PACK)) for h in range(2)]
+        nc.scalar.activation(*dealt[0], ACT.Copy)
+        nc.vector.tensor_copy(*dealt[1])
         query_codes = keep.tile([P, Q], U32, align_bytes=64)
         query_scales = keep.tile([P, Q], U8, align_bytes=64)
         for r in range(PACK):

from contextlib import ExitStack

import concourse.mybir as mybir
from concourse.masks import make_identity

D, E, T, I, Q = 512, 512, 1024, 256, 512
FLOPS = 2 * D * Q * I + 2 * Q * E * I

F32 = mybir.dt.float32
BF16 = mybir.dt.bfloat16
I32 = mybir.dt.int32
U32 = mybir.dt.uint32
U16 = mybir.dt.uint16
U8 = mybir.dt.uint8
FP8X4 = mybir.dt.float8_e4m3fn_x4
FP4X4 = mybir.dt.float4_e2m1fn_x4
ALU = mybir.AluOpType
ACT = mybir.ActivationFunctionType
AX = mybir.AxisListType

P = 128
PACK = 4
BANK = 512
E_TILES = E // P
T_BLOCKS = T // P
FADE_ROW, GB_ROW, SG_ROW, VEC_ROWS = 0, 8, 12, 16


def tile_attend_bvgatedby_s_kernel(tc, query, qs, grows, vals, keys_words, keys_scales, gates, gb, sg, old, fade, offs, out):
    nc = tc.nc
    with ExitStack() as ctx:
        keep = ctx.enter_context(tc.tile_pool(name="keep", bufs=1))
        ring = ctx.enter_context(tc.tile_pool(name="ring", bufs=2))
        psum = ctx.enter_context(tc.psum_pool(name="psum", bufs=1))

        def bank(n, name):
            return psum.tile([P, BANK], F32, tag="bank%d" % n, name=name)

        key_scales = keep.tile([P, T], U8, align_bytes=64)
        nc.gpsimd.memset(key_scales[:].bitcast(I32), 0)
        ident = keep.tile([P, P], F32)
        vec_rows = keep.tile([P, P], F32)
        nc.gpsimd.memset(vec_rows[:], 0.0)
        make_identity(nc, ident[:])

        offsets = keep.tile([P, I // 16], U16, name="offsets")
        nc.sync.dma_start(offsets[:], offs)
        key_words = keep.tile([P, T], U16, align_bytes=64)
        nc.sync.dma_start(key_words[:].bitcast(I32), keys_words[0].bitcast(I32))
        for quad in range(4):
            nc.sync.dma_start(key_scales[32 * quad : 32 * quad + 4, :].bitcast(I32),
                                keys_scales[0, 4 * quad : 4 * quad + 4, :].bitcast(I32))
        query_rows = query.rearrange("(p j) q -> p j q", j=PACK)
        query_raw = []
        for h in range(2):
            raw = keep.tile([P, PACK, Q // 2], F32, name="query_raw%d" % h)
            nc.sync.dma_start(raw[:], query_rows[:, :, h * (Q // 2) : (h + 1) * (Q // 2)])
            query_raw.append(raw)
        grows_rows = grows.rearrange("(p j) e -> p j e", j=PACK)
        grows_raw = []
        for h in range(2):
            raw = keep.tile([P, PACK, E // 2], F32, name="grows_raw%d" % h)
            nc.sync.dma_start(raw[:], grows_rows[:, :, h * (E // 2) : (h + 1) * (E // 2)])
            grows_raw.append(raw)
        row_scale = keep.tile([P, PACK], F32)
        nc.sync.dma_start(row_scale[:], qs.rearrange("(p r) o -> p (r o)", r=PACK))
        nc.sync.dma_start(vec_rows[SG_ROW : SG_ROW + I // P, :], sg.rearrange("o (c p) -> (o c) p", p=P))
        nc.sync.dma_start(vec_rows[GB_ROW : GB_ROW + E_TILES, :], gb.rearrange("(c p) o -> c (p o)", p=P))
        nc.sync.dma_start(vec_rows[FADE_ROW : FADE_ROW + T_BLOCKS, :], fade.rearrange("o (c p) -> (o c) p", p=P))
        gates_sb, vals_sb, old_sb = [], [], []
        for k in range(E_TILES):
            rows = slice(k * P, (k + 1) * P)
            for name, src, held in (("gates", gates, gates_sb), ("vals", vals, vals_sb), ("old", old, old_sb)):
                pool_tile = keep.tile([P, T], F32, name="%s%d" % (name, k))
                nc.sync.dma_start(pool_tile[:], src[rows, :])
                held.append(pool_tile)

        window = keep.tile([P, T], F32)
        nc.vector.memset(window[:], 0.0)

        listed_words = keep.tile([P, I], U16, align_bytes=64)
        listed_scales = keep.tile([P, I], U8, align_bytes=64)
        nc.vector.tensor_copy(listed_words[:], key_words[:].indirect(offsets[:]))
        nc.vector.tensor_copy(listed_scales[:], key_scales[:].indirect(offsets[:]))

        query_bf = keep.tile([P, PACK, P, PACK], BF16, align_bytes=64)
        half_s = P // 2
        dealt = [(query_bf[:, :, h * half_s : (h + 1) * half_s, :].rearrange("p r s j -> p s j r"),
                  query_raw[h][:].rearrange("p j (s r) -> p s j r", r=PACK)) for h in range(2)]
        nc.scalar.activation(*dealt[0], ACT.Copy)
        nc.vector.tensor_copy(*dealt[1])
        query_codes = keep.tile([P, Q], U32, align_bytes=64)
        query_scales = keep.tile([P, Q], U8, align_bytes=64)
        for r in range(PACK):
            cols = slice(r * P, (r + 1) * P)
            nc.vector.quantize_mx(query_codes[:, cols].bitcast(FP8X4), query_scales[:, cols],
                                  query_bf[:, r, :, :].rearrange("p s j -> p (s j)"))

        grows_bf = keep.tile([P, E, PACK], BF16, align_bytes=64)
        grows_codes = keep.tile([P, E], U32, align_bytes=64)
        grows_scales = keep.tile([P, E], U8, align_bytes=64)

        def cast_grows(k):
            src = grows_raw[k // 2][:, :, (k % 2) * P : (k % 2 + 1) * P]
            nc.scalar.copy(grows_bf[:, k * P : (k + 1) * P, :].rearrange("p (c i) j -> p c j i", i=4),
                           src.rearrange("p j (c i) -> p c j i", i=4))

        def quantize_grows(k):
            cols = slice(k * P, (k + 1) * P)
            nc.vector.quantize_mx(grows_codes[:, cols].bitcast(FP8X4), grows_scales[:, cols],
                                  grows_bf[:, cols, :].rearrange("p e j -> p (e j)"))

        cast_grows(0)
        cast_grows(1)

        neg_max = keep.tile([P, PACK], F32)
        row_sum = keep.tile([P, PACK], F32)
        inv_sum = keep.tile([P, PACK], F32)
        probs = keep.tile([P, PACK, I], F32)
        w_planes = keep.tile([P, PACK, I], BF16)
        scores = []
        for r in range(PACK):
            cols = slice(r * P, (r + 1) * P)
            score = bank(4 + r, "score%d" % r)
            nc.tensor.matmul_mx(score[:, :I], lhsT=query_codes[:, cols].bitcast(FP8X4), lhsT_scale=query_scales[:, cols],
                                rhs=listed_words[:].bitcast(FP4X4), rhs_scale=listed_scales[:], start=True, stop=True)
            scores.append(score)
        for r in range(PACK):
            nc.vector.tensor_reduce(neg_max[:, r : r + 1], scores[r][:, :I], AX.X, ALU.max, negate=True)
            nc.scalar.activation(probs[:, r, :], scores[r][:, :I], ACT.Exp, bias=neg_max[:, r : r + 1],
                                 accum_out=row_sum[:, r : r + 1])
        for r in range(PACK):
            nc.vector.reciprocal(inv_sum[:, r : r + 1], row_sum[:, r : r + 1])
            if r < 2:
                quantize_grows(r)
            nc.vector.tensor_scalar(w_planes[:, r, :], probs[:, r, :], inv_sum[:, r : r + 1], row_scale[:, r : r + 1],
                                    ALU.mult, ALU.mult)
        w_bf = keep.tile([P, I, PACK], BF16, align_bytes=64)
        nc.vector.tensor_copy(w_bf[:].rearrange("p (c i) r -> p c r i", i=4),
                              w_planes[:].rearrange("p r (c i) -> p c r i", i=4))
        w_codes = keep.tile([P, I], U32, align_bytes=64)
        w_scales = keep.tile([P, I], U8, align_bytes=64)
        nc.vector.quantize_mx(w_codes[:].bitcast(FP8X4), w_scales[:], w_bf[:].rearrange("p i r -> p (i r)"))

        turned = bank(7, "turned")
        nc.tensor.transpose(turned[:, :P], vec_rows[:], ident[:])
        vec_cols = keep.tile([P, VEC_ROWS], F32)
        nc.scalar.copy(vec_cols[:], turned[:, :VEC_ROWS])
        spread = bank(3, "spread")
        for c in range(I // P):
            nc.tensor.transpose(spread[:, c * P : (c + 1) * P],
                                vec_cols[:, SG_ROW + c : SG_ROW + c + 1].to_broadcast([P, P]), ident[:])
        neg_gain = keep.tile([P, I], F32)
        nc.scalar.activation(neg_gain[:], spread[:, :I], ACT.Copy, scale=-0.25)
        half_bias = keep.tile([P, E_TILES], F32)
        nc.scalar.activation(half_bias[:], turned[:, GB_ROW : GB_ROW + E_TILES], ACT.Copy, scale=0.5)

        for k in range(E_TILES):
            cols = slice(k * P, (k + 1) * P)
            if k >= 2:
                cast_grows(k)
                quantize_grows(k)
            c0 = bank(k % 2, "c0_%d" % k)
            nc.tensor.matmul_mx(c0[:, :I], lhsT=grows_codes[:, cols].bitcast(FP8X4), lhsT_scale=grows_scales[:, cols],
                                rhs=w_codes[:].bitcast(FP8X4), rhs_scale=w_scales[:], start=True, stop=True)
            listed_gates = ring.tile([P, I], F32, name="listed_gates")
            nc.vector.tensor_copy(listed_gates[:], gates_sb[k][:].indirect(offsets[:]))
            tanh_half = ring.tile([P, I], F32, name="tanh_half")
            nc.scalar.activation(tanh_half[:], listed_gates[:], ACT.Tanh, bias=half_bias[:, k : k + 1], scale=0.5)
            centred = ring.tile([P, I], F32, name="centred")
            nc.scalar.activation(centred[:], tanh_half[:], ACT.Square)
            gained = ring.tile([P, I], F32, name="gained")
            nc.vector.tensor_tensor(gained[:], vals_sb[k][:].indirect(offsets[:]), neg_gain[:], ALU.mult)
            chained = ring.tile([P, I], F32, name="chained")
            nc.vector.scalar_tensor_tensor(chained[:], centred[:], -1.0, c0[:, :I], ALU.add, ALU.mult)
            nc.vector.tensor_tensor(window[:].indirect(offsets[:]), gained[:], chained[:], ALU.mult)

            faded_t = ring.tile([P, T_BLOCKS, P], F32, name="faded_t")
            for half in range(2):
                old_t = bank(2 + half, "old_t%d_%d" % (k, half))
                for c in range(4):
                    blk = 4 * half + c
                    nc.tensor.transpose(old_t[:, c * P : (c + 1) * P], old_sb[k][:, blk * P : (blk + 1) * P], ident[:])
                for c in range(4):
                    blk = 4 * half + c
                    nc.scalar.activation(faded_t[:, blk, :], old_t[:, c * P : (c + 1) * P], ACT.Copy,
                                         scale=vec_cols[:, FADE_ROW + blk : FADE_ROW + blk + 1])
            for half in range(2):
                faded = bank(4 + 2 * (k % 2) + half, "faded%d_%d" % (k, half))
                for c in range(4):
                    nc.tensor.transpose(faded[:, c * P : (c + 1) * P], faded_t[:, 4 * half + c, :], ident[:])
                result = keep.tile([P, BANK], F32, name="result%d_%d" % (k, half))
                t_cols = slice(half * BANK, (half + 1) * BANK)
                nc.vector.tensor_tensor(result[:], faded[:], window[:, t_cols], ALU.add)
                nc.sync.dma_start(out[cols, t_cols], result[:])
